import numpy as np
import ml_dtypes


def mxq(x, axis, fmt="e4m3"):
    dtype, down = {"e4m3": (ml_dtypes.float8_e4m3fn, 7), "e5m2": (ml_dtypes.float8_e5m2, 14)}[fmt]
    v = np.moveaxis(np.asarray(x, np.float32).astype(ml_dtypes.bfloat16).astype(np.float64), axis, -1)
    blocks = v.reshape(v.shape[:-1] + (-1, 32))
    amax = np.abs(blocks).max(-1, keepdims=True)
    byte = np.maximum(np.where(amax > 0, np.frexp(amax)[1] - 1 + 127, 0) - down, 1)
    scale = np.exp2(byte - 127.0)
    codes = (blocks / scale).astype(np.float32).astype(dtype).astype(np.float64)
    return np.moveaxis((codes * scale).reshape(v.shape), -1, axis)


WIDE = False


def mx_kscale(k):
    if not WIDE:
        return np.ones(k)
    levels = np.array([10, -10, 5, -5, 0])
    if k % 512:
        return np.exp2(np.random.permutation(np.resize(levels, k // 32))).repeat(32)
    a = np.empty((k // 512, 16))
    for p in range(k // 512):
        a[p, :8] = np.random.permutation(np.resize(levels, 8))
        for g in range(8):
            far = levels[np.abs(levels - a[p, g]) >= 10]
            a[p, g + 8] = far[np.random.randint(len(far))]
    return np.exp2(a.ravel()).repeat(32)


def f64(x):
    return np.asarray(x).astype(np.float64)


def striped(idx):
    return np.tile(idx.reshape(-1, 16).T, (8, 1)).astype(np.uint16)


def unstriped(offs):
    return offs[:16].T.reshape(-1).astype(np.int64)


def striped8(idx):
    return np.concatenate([x.reshape(-1, 16).T for x in idx]).astype(np.uint16)


def runs(offs, k):
    lists = np.stack([offs[16 * r : 16 * r + 16].T.reshape(-1) for r in range(8)]).astype(np.int64)
    return lists[np.arange(k) % 512 // 64]


def pack_weight(w):
    k, n = w.shape
    w = f64(np.asarray(w, np.float32).astype(ml_dtypes.bfloat16)).reshape(k // 32, 32, n)
    amax = np.abs(w).max(1)
    byte = np.clip(np.where(amax > 0, np.frexp(amax)[1] - 1 + 127 - 7, 1), 1, 254)
    scaled = (w * np.exp2(127.0 - byte)[:, None, :]).reshape(k, n).astype(np.float32)
    words = np.ascontiguousarray(scaled.reshape(k // 512, 128, 4, n).transpose(0, 1, 3, 2)).astype(ml_dtypes.float8_e4m3fn).view(np.uint8)
    return words, np.ascontiguousarray(byte.astype(np.uint8).reshape(k // 512, 16, n))


def unpack_weight(words, scales):
    g, p, n, _ = words.shape
    vals = np.ascontiguousarray(words).view(ml_dtypes.float8_e4m3fn).astype(np.float64) * np.repeat(np.exp2(scales.astype(np.float64) - 127.0), 8, axis=1)[..., None]
    return vals.transpose(0, 1, 3, 2).reshape(g * 512, n)


def sigmoid(v):
    return 1.0 / (1.0 + np.exp(-np.maximum(v, -700.0)))


K, T, S, N, H = 512, 2048, 512, 512, 512


def setup_inputs():
    n = np.random.standard_normal
    s = mx_kscale(K)[:, None]
    u = mx_kscale(H)
    packed_xT = pack_weight(n((K, T)) * s)
    return {
        "x_words": packed_xT[0],
        "x_scales": packed_xT[1],
        "w1": (n((K, H)) / np.sqrt(K) / s).astype(np.float32),
        "w2": (n((K, H)) / np.sqrt(K) / s).astype(np.float32),
        "w3": (n((K, H)) / np.sqrt(K) / s).astype(np.float32),
        "gn": (np.random.uniform(0.5, 1.5, (H, 1)) * u[:, None]).astype(np.float32),
        "w4": (n((H, N)) / np.sqrt(H) / u[:, None]).astype(np.float32),
        "offs": striped(np.random.permutation(T)[:S]),
        "two": striped(np.random.permutation(T)[:S]),
        "three": striped(np.random.permutation(T)[:S]),
        "n1": striped8(np.stack([np.random.permutation(S) for _ in range(8)])),
        "n2": striped8(np.stack([np.random.permutation(S) for _ in range(8)])),
        "n3": striped8(np.stack([np.random.permutation(S) for _ in range(8)])),
        "n4": striped8(np.stack([np.random.permutation(S) for _ in range(8)])),
        "n5": striped8(np.stack([np.random.permutation(S) for _ in range(8)])),
        "n6": striped8(np.stack([np.random.permutation(S) for _ in range(8)])),
        "n7": striped8(np.stack([np.random.permutation(S) for _ in range(8)])),
    }


def reference(x_words, x_scales, w1, w2, w3, gn, w4, offs, two, three, n1, n2, n3, n4, n5, n6, n7):
    x_three = unpack_weight(x_words, x_scales)[:, unstriped(three)]
    b = mxq(f64(w3), 0, "e4m3").T @ x_three
    xq = unpack_weight(x_words, x_scales)[:, unstriped(offs)]
    y = mxq(f64(w1), 0, "e4m3").T @ xq
    x_two = unpack_weight(x_words, x_scales)[:, unstriped(two)]
    d = mxq(f64(w2), 0, "e4m3").T @ x_two
    m1 = y * (sigmoid(d[np.arange(H)[:, None], runs(n2, H)])) - (0.5 * (y[np.arange(H)[:, None], runs(n1, H)]))
    z = f64(gn) * (b * (m1[np.arange(H)[:, None], runs(n3, H)] - m1) + 0.5 * ((b[np.arange(H)[:, None], runs(n5, H)]) * (m1[np.arange(H)[:, None], runs(n4, H)] - m1)))
    h = mxq(f64(w4), 0, "e4m3").T @ mxq(z, 0, "e4m3")
    pa = h[np.arange(N)[:, None], runs(n6, N)]
    pb = h[np.arange(N)[:, None], runs(n7, N)]
    return np.maximum(np.minimum(h, pa), np.minimum(np.maximum(h, pa), pb))

@@ -1,0 +1,233 @@
+from contextlib import ExitStack
+
+import concourse.mybir as mybir
+
+F32 = mybir.dt.float32
+BF16 = mybir.dt.bfloat16
+I32 = mybir.dt.int32
+U32 = mybir.dt.uint32
+U16 = mybir.dt.uint16
+U8 = mybir.dt.uint8
+FP8X4 = mybir.dt.float8_e4m3fn_x4
+ALU = mybir.AluOpType
+ACT = mybir.ActivationFunctionType
+
+P = 128
+PACK = 4
+T = 2048
+S = 512
+FLOPS = 4 * 2 * 512 * 512 * 512
+
+
+def tile_picked_triogatebflowbmed_none_p_kernel(
+    tc, x_words, x_scales, w1, w2, w3, gn, w4, offs, two, three, n1, n2, n3, n4, n5, n6, n7, out
+):
+    nc = tc.nc
+    with ExitStack() as ctx:
+        lists = ctx.enter_context(tc.tile_pool(name="lists", bufs=1))
+        keep = ctx.enter_context(tc.tile_pool(name="keep", bufs=1))
+        ring = ctx.enter_context(tc.tile_pool(name="ring", bufs=2))
+        psum = ctx.enter_context(tc.psum_pool(name="psum", bufs=2))
+
+        def load_list(src, name):
+            tile = lists.tile([P, S // 16], U16, name=name)
+            nc.sync.dma_start(tile[:], src)
+            return tile
+
+        def load_weight(src, name, parts):
+            rows = src.rearrange("(p j) c -> p j c", j=PACK)
+            width = S // parts
+            raws = []
+            for part in range(parts):
+                raw = keep.tile([P, PACK, width], F32, name="%s_raw%d" % (name, part))
+                nc.sync.dma_start(out=raw[:], in_=rows[:, :, part * width : (part + 1) * width])
+                raws.append(raw)
+            return raws
+
+        def deal_part(dealt, raws, part):
+            span = P // len(raws)
+            nc.scalar.copy(
+                out=dealt[:].rearrange("p (t m j) -> p m j t", t=PACK, j=PACK)[:, part * span : (part + 1) * span],
+                in_=raws[part][:].rearrange("p j (m t) -> p m j t", t=PACK),
+            )
+
+        def deal_weight(raws, name):
+            dealt = keep.tile([P, PACK * S], BF16, name=name + "_dealt", align_bytes=64)
+            for part in range(len(raws)):
+                deal_part(dealt, raws, part)
+            return dealt
+
+        def quantize(values, name):
+            codes = keep.tile([P, S], U32, name=name + "_codes", align_bytes=64)
+            scales = keep.tile([P, S], U8, name=name + "_scales", align_bytes=64)
+            nc.vector.quantize_mx(out=codes[:].bitcast(FP8X4), scales=scales[:], in_=values[:])
+            return codes, scales
+
+        def product(weight, moving, t, tag):
+            acc = psum.tile([P, S], F32, name=tag)
+            cols = slice(t * P, (t + 1) * P)
+            nc.tensor.matmul_mx(
+                out=acc[:],
+                lhsT=weight[0][:, cols].bitcast(FP8X4),
+                lhsT_scale=weight[1][:, cols],
+                rhs=moving[0][:].bitcast(FP8X4),
+                rhs_scale=moving[1][:],
+                start=True,
+                stop=True,
+            )
+            return acc
+
+        byte_table = keep.tile([P, T], U8, name="byte_table")
+        nc.gpsimd.memset(byte_table[:].bitcast(I32), 0)
+        warm = keep.tile([P, 2], F32, name="warm")
+        nc.gpsimd.memset(warm[:, 0:1], 0.0)
+        nc.scalar.activation(out=warm[:, 1:2], in_=warm[:, 0:1], func=ACT.Sigmoid)
+
+        two_l = load_list(two, "two_l")
+        offs_l = load_list(offs, "offs_l")
+        for q in range(4):
+            nc.sync.dma_start(
+                out=byte_table[32 * q : 32 * q + 4, :].bitcast(I32),
+                in_=x_scales[0, 4 * q : 4 * q + 4, :].bitcast(I32),
+            )
+        word_table = keep.tile([P, T], I32, name="word_table")
+        nc.sync.dma_start(out=word_table[:], in_=x_words[0].rearrange("p n r -> p (n r)").bitcast(I32))
+        w2_raw = load_weight(w2, "w2", 2)
+        w1_raw = load_weight(w1, "w1", 2)
+        three_l = load_list(three, "three_l")
+        n2_l = load_list(n2, "n2_l")
+        n1_l = load_list(n1, "n1_l")
+        w3_raw = load_weight(w3, "w3", 2)
+        n4_l = load_list(n4, "n4_l")
+        n3_l = load_list(n3, "n3_l")
+        n5_l = load_list(n5, "n5_l")
+        w4_raw = load_weight(w4, "w4", 1)
+        n6_l = load_list(n6, "n6_l")
+        n7_l = load_list(n7, "n7_l")
+        gain = keep.tile([P, PACK], F32, name="gain")
+        nc.gpsimd.dma_start(out=gain[:], in_=gn.rearrange("(p t) o -> p (t o)", t=PACK))
+        half_gain = keep.tile([P, PACK], F32, name="half_gain")
+        nc.gpsimd.tensor_scalar(half_gain[:], gain[:], 0.5, 0.0, ALU.mult, ALU.add)
+
+        def pick_bytes(lst, name):
+            picked = keep.tile([P, S], U8, name=name + "_bytes", align_bytes=64)
+            nc.vector.tensor_copy(picked[:], byte_table[:].indirect(lst[:]))
+            return picked
+
+        def pick_words(lst, name):
+            picked = keep.tile([P, S], U32, name=name, align_bytes=64)
+            nc.vector.tensor_copy(picked[:], word_table[:].bitcast(U32).indirect(lst[:]))
+            return picked
+
+        bytes_two = pick_bytes(two_l, "two")
+        bytes_offs = pick_bytes(offs_l, "offs")
+        x_two = (pick_words(two_l, "two_words"), bytes_two)
+        x_offs = (pick_words(offs_l, "offs_words"), bytes_offs)
+        w2_q = quantize(deal_weight(w2_raw, "w2"), "w2")
+        bytes_three = pick_bytes(three_l, "three")
+        w1_q = quantize(deal_weight(w1_raw, "w1"), "w1")
+        x_three = (pick_words(three_l, "w1_dealt"), bytes_three)
+
+        y_win = [keep.tile([P, 2 * S], F32, name="y_win%d" % t) for t in range(PACK)]
+        m_win = [keep.tile([P, 2 * S], F32, name="m_win%d" % t) for t in range(PACK)]
+        b_win = [keep.tile([P, 2 * S], F32, name="b_win%d" % t) for t in range(PACK)]
+        h_win = [keep.tile([P, 2 * S], F32, name="h_win%d" % t) for t in range(PACK)]
+        term_a = keep.tile([P, PACK, S], F32, name="term_a")
+        term_b = keep.tile([P, PACK, S], F32, name="term_b")
+        lo = slice(0, S)
+        hi = slice(S, 2 * S)
+
+        def gate(t):
+            d_acc = product(w2_q, x_two, t, "d_acc")
+            y_acc = product(w1_q, x_offs, t, "y_acc")
+            d_win = ring.tile([P, S], F32, name="d_win")
+            nc.scalar.copy(out=d_win[:], in_=d_acc[:])
+            for half in range(2):
+                nc.scalar.activation(
+                    out=y_win[t][:, S + half * 256 : S + (half + 1) * 256],
+                    in_=d_win[:].indirect(n2_l[:, half * 16 : (half + 1) * 16]),
+                    func=ACT.Sigmoid,
+                )
+            nc.scalar.activation(out=y_win[t][:, lo], in_=y_acc[:], func=ACT.Copy, scale=-0.5)
+            nc.vector.tensor_tensor(m_win[t][:, hi], y_acc[:], y_win[t][:, hi], ALU.mult)
+            nc.vector.tensor_tensor(m_win[t][:, lo], y_win[t][:].indirect(n1_l[:]), m_win[t][:, hi], ALU.add)
+
+        pull3 = [keep.tile([P, S], F32, name="pull3_%d" % t) for t in range(PACK)]
+
+        def pulls(t):
+            nc.scalar.copy(out=b_win[t][:, hi], in_=m_win[t][:, lo])
+            nc.vector.tensor_tensor(h_win[t][:, hi], m_win[t][:].indirect(n4_l[:]), b_win[t][:, hi], ALU.subtract)
+            nc.vector.tensor_tensor(pull3[t][:], m_win[t][:].indirect(n3_l[:]), b_win[t][:, hi], ALU.subtract)
+
+        def terms(t):
+            b_acc = product(w3_q, x_three, t, "b_acc")
+            nc.scalar.activation(out=b_win[t][:, lo], in_=b_acc[:], func=ACT.Copy, scale=half_gain[:, t : t + 1])
+            nc.vector.tensor_tensor(term_b[:, t, :], b_win[t][:].indirect(n5_l[:]), h_win[t][:, hi], ALU.mult)
+            nc.vector.scalar_tensor_tensor(term_a[:, t, :], pull3[t][:], 2.0, b_win[t][:, lo], ALU.mult, ALU.mult)
+
+        gate(0)
+        gate(1)
+        w3_dealt = keep.tile([P, PACK * S], BF16, name="w3_dealt", align_bytes=64)
+        pulls(0)
+        deal_part(w3_dealt, w3_raw, 0)
+        pulls(1)
+        deal_part(w3_dealt, w3_raw, 1)
+        w3_q = quantize(w3_dealt, "w3")
+        gate(2)
+        terms(0)
+        terms(1)
+        gate(3)
+        pulls(2)
+        terms(2)
+        pulls(3)
+        terms(3)
+        w4_q = quantize(deal_weight(w4_raw, "w4"), "w4")
+
+        z = keep.tile([P, S * PACK], BF16, name="z", align_bytes=64)
+        z_codes = keep.tile([P, S], U32, name="z_codes", align_bytes=64)
+        z_scales = keep.tile([P, S], U8, name="z_scales", align_bytes=64)
+        halves = [slice(0, S // 2), slice(S // 2, S)]
+        for cols in halves:
+            nc.vector.tensor_tensor(
+                z[:, PACK * cols.start : PACK * cols.stop].rearrange("p (c i t) -> p c t i", i=4, t=PACK),
+                term_a[:, :, cols].rearrange("p t (c i) -> p c t i", i=4),
+                term_b[:, :, cols].rearrange("p t (c i) -> p c t i", i=4),
+                ALU.add,
+            )
+        for cols in halves:
+            nc.vector.quantize_mx(
+                out=z_codes[:, cols].bitcast(FP8X4), scales=z_scales[:, cols], in_=z[:, PACK * cols.start : PACK * cols.stop]
+            )
+
+        out_rows = out.rearrange("(p t) j -> p t j", t=PACK)
+        for t in range(PACK):
+            h_own = ring.tile([P, S], F32, name="h_own")
+            for cols in halves if t == 0 else [lo]:
+                h_acc = psum.tile([P, S], F32, name="h_acc")
+                width = cols.stop - cols.start
+                nc.tensor.matmul_mx(
+                    out=h_acc[:, 0:width],
+                    lhsT=w4_q[0][:, t * P : (t + 1) * P].bitcast(FP8X4),
+                    lhsT_scale=w4_q[1][:, t * P : (t + 1) * P],
+                    rhs=z_codes[:, cols].bitcast(FP8X4),
+                    rhs_scale=z_scales[:, cols],
+                    start=True,
+                    stop=True,
+                )
+                nc.scalar.copy(out=h_win[t][:, cols], in_=h_acc[:, 0:width])
+                nc.scalar.copy(out=h_own[:, cols], in_=h_acc[:, 0:width])
+            step_a = ring.tile([P, S], F32, name="step_a")
+            step_b = ring.tile([P, S], F32, name="step_b")
+            nc.vector.tensor_tensor(step_a[:], h_win[t][:].indirect(n6_l[:]), h_own[:], ALU.subtract)
+            nc.vector.tensor_tensor(step_b[:], h_win[t][:].indirect(n7_l[:]), h_own[:], ALU.subtract)
+            upper = ring.tile([P, S], F32, name="upper")
+            middle = ring.tile([P, S], F32, name="middle")
+            result = ring.tile([P, S], F32, name="result")
+            pieces = halves if t == PACK - 1 else [lo]
+            for cols in pieces:
+                nc.vector.scalar_tensor_tensor(upper[:, cols], step_a[:, cols], 0.0, step_b[:, cols], ALU.max, ALU.min)
+            for cols in pieces:
+                nc.vector.scalar_tensor_tensor(middle[:, cols], step_a[:, cols], 0.0, upper[:, cols], ALU.min, ALU.max)
+            for cols in pieces:
+                nc.vector.tensor_tensor(result[:, cols], middle[:, cols], h_own[:, cols], ALU.add)
+                nc.sync.dma_start(out=out_rows[:, t, cols], in_=result[:, cols])

@@ -1,6 +1,7 @@
 from contextlib import ExitStack
 
 import concourse.mybir as mybir
+from concourse.masks import make_identity
 
 F32 = mybir.dt.float32
 BF16 = mybir.dt.bfloat16
@@ -16,7 +17,14 @@ P = 128
 PACK = 4
 T = 2048
 S = 512
-FLOPS = 4 * 2 * 512 * 512 * 512
+STRIPE = 16
+QUADRANT = 32
+FLOPS = 4 * 2 * S * S * S
+
+WHOLE = slice(0, S)
+SPARE = slice(S, 2 * S)
+HALVES = [slice(0, S // 2), slice(S // 2, S)]
+Z_PARTS = [slice(0, 256), slice(256, 384), slice(384, S)]
 
 
 def tile_picked_triogatebflowbmed_none_p_kernel(
@@ -27,19 +35,23 @@ def tile_picked_triogatebflowbmed_none_p_kernel(
         lists = ctx.enter_context(tc.tile_pool(name="lists", bufs=1))
         keep = ctx.enter_context(tc.tile_pool(name="keep", bufs=1))
         ring = ctx.enter_context(tc.tile_pool(name="ring", bufs=2))
-        psum = ctx.enter_context(tc.psum_pool(name="psum", bufs=2))
+        psum_pairs = ctx.enter_context(tc.psum_pool(name="psum_pairs", bufs=2))
+        psum_single = ctx.enter_context(tc.psum_pool(name="psum_single", bufs=1))
 
-        def load_list(src, name):
-            tile = lists.tile([P, S // 16], U16, name=name)
-            nc.sync.dma_start(tile[:], src)
+        def load_list(source, name):
+            tile = lists.tile([P, S // STRIPE], U16, name=name)
+            nc.sync.dma_start(tile[:], source)
             return tile
 
-        def load_weight(src, name, parts):
-            rows = src.rearrange("(p j) c -> p j c", j=PACK)
+        def entries(list_tile, places):
+            return list_tile[:, places.start // STRIPE : places.stop // STRIPE]
+
+        def load_weight(source, name, parts):
+            rows = source.rearrange("(p j) c -> p j c", j=PACK)
             width = S // parts
             raws = []
             for part in range(parts):
-                raw = keep.tile([P, PACK, width], F32, name="%s_raw%d" % (name, part))
+                raw = keep.tile([P, PACK, width], F32, name="%s_raw%d" % (name, part), align_bytes=64)
                 nc.sync.dma_start(out=raw[:], in_=rows[:, :, part * width : (part + 1) * width])
                 raws.append(raw)
             return raws
@@ -63,15 +75,15 @@ def tile_picked_triogatebflowbmed_none_p_kernel(
             nc.vector.quantize_mx(out=codes[:].bitcast(FP8X4), scales=scales[:], in_=values[:])
             return codes, scales
 
-        def product(weight, moving, t, tag):
-            acc = psum.tile([P, S], F32, name=tag)
+        def product(weight, picked, t, pool, bank):
+            acc = pool.tile([P, S], F32, name=bank)
             cols = slice(t * P, (t + 1) * P)
             nc.tensor.matmul_mx(
                 out=acc[:],
                 lhsT=weight[0][:, cols].bitcast(FP8X4),
                 lhsT_scale=weight[1][:, cols],
-                rhs=moving[0][:].bitcast(FP8X4),
-                rhs_scale=moving[1][:],
+                rhs=picked[0][:].bitcast(FP8X4),
+                rhs_scale=picked[1][:],
                 start=True,
                 stop=True,
             )
@@ -79,95 +91,95 @@ def tile_picked_triogatebflowbmed_none_p_kernel(
 
         byte_table = keep.tile([P, T], U8, name="byte_table")
         nc.gpsimd.memset(byte_table[:].bitcast(I32), 0)
-        warm = keep.tile([P, 2], F32, name="warm")
-        nc.gpsimd.memset(warm[:, 0:1], 0.0)
-        nc.scalar.activation(out=warm[:, 1:2], in_=warm[:, 0:1], func=ACT.Sigmoid)
+        identity = keep.tile([P, P], F32, name="identity")
+        make_identity(nc, identity[:])
 
         two_l = load_list(two, "two_l")
         offs_l = load_list(offs, "offs_l")
-        for q in range(4):
+        for q in range(P // QUADRANT):
             nc.sync.dma_start(
-                out=byte_table[32 * q : 32 * q + 4, :].bitcast(I32),
-                in_=x_scales[0, 4 * q : 4 * q + 4, :].bitcast(I32),
+                out=byte_table[QUADRANT * q : QUADRANT * q + PACK, :].bitcast(I32),
+                in_=x_scales[0, PACK * q : PACK * (q + 1), :].bitcast(I32),
             )
+        three_l = load_list(three, "three_l")
+        w2_raw = load_weight(w2, "w2", 2)
         word_table = keep.tile([P, T], I32, name="word_table")
         nc.sync.dma_start(out=word_table[:], in_=x_words[0].rearrange("p n r -> p (n r)").bitcast(I32))
-        w2_raw = load_weight(w2, "w2", 2)
         w1_raw = load_weight(w1, "w1", 2)
-        three_l = load_list(three, "three_l")
         n2_l = load_list(n2, "n2_l")
         n1_l = load_list(n1, "n1_l")
         w3_raw = load_weight(w3, "w3", 2)
         n4_l = load_list(n4, "n4_l")
         n3_l = load_list(n3, "n3_l")
         n5_l = load_list(n5, "n5_l")
+        gain = keep.tile([P, PACK], F32, name="gain")
+        nc.sync.dma_start(out=gain[:], in_=gn.rearrange("(p t) o -> p (t o)", t=PACK))
         w4_raw = load_weight(w4, "w4", 1)
         n6_l = load_list(n6, "n6_l")
         n7_l = load_list(n7, "n7_l")
-        gain = keep.tile([P, PACK], F32, name="gain")
-        nc.gpsimd.dma_start(out=gain[:], in_=gn.rearrange("(p t) o -> p (t o)", t=PACK))
-        half_gain = keep.tile([P, PACK], F32, name="half_gain")
-        nc.gpsimd.tensor_scalar(half_gain[:], gain[:], 0.5, 0.0, ALU.mult, ALU.add)
 
-        def pick_bytes(lst, name):
+        def pick_bytes(list_tile, name):
             picked = keep.tile([P, S], U8, name=name + "_bytes", align_bytes=64)
-            nc.vector.tensor_copy(picked[:], byte_table[:].indirect(lst[:]))
+            nc.vector.tensor_copy(picked[:], byte_table[:].indirect(list_tile[:]))
             return picked
 
-        def pick_words(lst, name):
-            picked = keep.tile([P, S], U32, name=name, align_bytes=64)
-            nc.vector.tensor_copy(picked[:], word_table[:].bitcast(U32).indirect(lst[:]))
+        def pick_words(list_tile, name):
+            picked = keep.tile([P, S], U32, name=name + "_words", align_bytes=64)
+            nc.vector.tensor_copy(picked[:], word_table[:].bitcast(U32).indirect(list_tile[:]))
             return picked
 
         bytes_two = pick_bytes(two_l, "two")
         bytes_offs = pick_bytes(offs_l, "offs")
-        x_two = (pick_words(two_l, "two_words"), bytes_two)
-        x_offs = (pick_words(offs_l, "offs_words"), bytes_offs)
-        w2_q = quantize(deal_weight(w2_raw, "w2"), "w2")
         bytes_three = pick_bytes(three_l, "three")
+        w2_q = quantize(deal_weight(w2_raw, "w2"), "w2")
+        x_two = (pick_words(two_l, "two"), bytes_two)
+        x_offs = (pick_words(offs_l, "offs"), bytes_offs)
+        x_three = (pick_words(three_l, "three"), bytes_three)
         w1_q = quantize(deal_weight(w1_raw, "w1"), "w1")
-        x_three = (pick_words(three_l, "w1_dealt"), bytes_three)
 
-        y_win = [keep.tile([P, 2 * S], F32, name="y_win%d" % t) for t in range(PACK)]
+        y_win = [keep.tile([P, 2 * S], F32, name="y_win%d" % t, align_bytes=64) for t in range(PACK)]
         m_win = [keep.tile([P, 2 * S], F32, name="m_win%d" % t) for t in range(PACK)]
         b_win = [keep.tile([P, 2 * S], F32, name="b_win%d" % t) for t in range(PACK)]
         h_win = [keep.tile([P, 2 * S], F32, name="h_win%d" % t) for t in range(PACK)]
+        pull3 = [keep.tile([P, S], F32, name="pull3_%d" % t) for t in range(PACK)]
         term_a = keep.tile([P, PACK, S], F32, name="term_a")
         term_b = keep.tile([P, PACK, S], F32, name="term_b")
-        lo = slice(0, S)
-        hi = slice(S, 2 * S)
+        d_slots = ["w1_raw1", "w1_dealt", "d_win2", "d_win3"]
 
         def gate(t):
-            d_acc = product(w2_q, x_two, t, "d_acc")
-            y_acc = product(w1_q, x_offs, t, "y_acc")
-            d_win = ring.tile([P, S], F32, name="d_win")
+            d_acc = product(w2_q, x_two, t, psum_pairs, "d_acc")
+            y_acc = product(w1_q, x_offs, t, psum_single, "y_acc")
+            d_win = keep.tile([P, S], F32, name=d_slots[t], align_bytes=64)
             nc.scalar.copy(out=d_win[:], in_=d_acc[:])
-            for half in range(2):
+            for places in HALVES:
                 nc.scalar.activation(
-                    out=y_win[t][:, S + half * 256 : S + (half + 1) * 256],
-                    in_=d_win[:].indirect(n2_l[:, half * 16 : (half + 1) * 16]),
+                    out=y_win[t][:, S + places.start : S + places.stop],
+                    in_=d_win[:].indirect(entries(n2_l, places)),
                     func=ACT.Sigmoid,
                 )
-            nc.scalar.activation(out=y_win[t][:, lo], in_=y_acc[:], func=ACT.Copy, scale=-0.5)
-            nc.vector.tensor_tensor(m_win[t][:, hi], y_acc[:], y_win[t][:, hi], ALU.mult)
-            nc.vector.tensor_tensor(m_win[t][:, lo], y_win[t][:].indirect(n1_l[:]), m_win[t][:, hi], ALU.add)
-
-        pull3 = [keep.tile([P, S], F32, name="pull3_%d" % t) for t in range(PACK)]
+            if t == 0:
+                nc.vector.tensor_scalar(y_win[t][:, WHOLE], y_acc[:], -0.25, None, ALU.mult)
+            else:
+                nc.scalar.activation(out=y_win[t][:, WHOLE], in_=y_acc[:], func=ACT.Copy, scale=-0.25)
+            for places in HALVES if t < 2 else [WHOLE]:
+                spare = slice(S + places.start, S + places.stop)
+                nc.vector.scalar_tensor_tensor(m_win[t][:, spare], y_acc[:, places], 0.5, y_win[t][:, spare], ALU.mult, ALU.mult)
+            nc.vector.tensor_tensor(m_win[t][:, WHOLE], y_win[t][:].indirect(n1_l[:]), m_win[t][:, SPARE], ALU.add)
 
         def pulls(t):
-            nc.scalar.copy(out=b_win[t][:, hi], in_=m_win[t][:, lo])
-            nc.vector.tensor_tensor(h_win[t][:, hi], m_win[t][:].indirect(n4_l[:]), b_win[t][:, hi], ALU.subtract)
-            nc.vector.tensor_tensor(pull3[t][:], m_win[t][:].indirect(n3_l[:]), b_win[t][:, hi], ALU.subtract)
+            nc.scalar.copy(out=b_win[t][:, SPARE], in_=m_win[t][:, WHOLE])
+            nc.vector.tensor_tensor(h_win[t][:, SPARE], m_win[t][:].indirect(n4_l[:]), b_win[t][:, SPARE], ALU.subtract)
+            nc.vector.tensor_tensor(pull3[t][:], m_win[t][:].indirect(n3_l[:]), b_win[t][:, SPARE], ALU.subtract)
 
         def terms(t):
-            b_acc = product(w3_q, x_three, t, "b_acc")
-            nc.scalar.activation(out=b_win[t][:, lo], in_=b_acc[:], func=ACT.Copy, scale=half_gain[:, t : t + 1])
-            nc.vector.tensor_tensor(term_b[:, t, :], b_win[t][:].indirect(n5_l[:]), h_win[t][:, hi], ALU.mult)
-            nc.vector.scalar_tensor_tensor(term_a[:, t, :], pull3[t][:], 2.0, b_win[t][:, lo], ALU.mult, ALU.mult)
+            b_acc = product(w3_q, x_three, t, psum_pairs, "b_acc")
+            nc.scalar.activation(out=b_win[t][:, WHOLE], in_=b_acc[:], func=ACT.Copy, scale=gain[:, t : t + 1])
+            nc.vector.tensor_tensor(term_b[:, t, :], b_win[t][:].indirect(n5_l[:]), h_win[t][:, SPARE], ALU.mult)
+            nc.vector.scalar_tensor_tensor(term_a[:, t, :], pull3[t][:], 2.0, b_win[t][:, WHOLE], ALU.mult, ALU.mult)
 
         gate(0)
         gate(1)
-        w3_dealt = keep.tile([P, PACK * S], BF16, name="w3_dealt", align_bytes=64)
+        w3_dealt = keep.tile([P, PACK * S], BF16, name="y_win0", align_bytes=64)
         pulls(0)
         deal_part(w3_dealt, w3_raw, 0)
         pulls(1)
@@ -181,53 +193,97 @@ def tile_picked_triogatebflowbmed_none_p_kernel(
         terms(2)
         pulls(3)
         terms(3)
-        w4_q = quantize(deal_weight(w4_raw, "w4"), "w4")
+        w4_dealt = keep.tile([P, PACK * S], BF16, name="y_win3", align_bytes=64)
+        deal_part(w4_dealt, w4_raw, 0)
+        first_codes = keep.tile([P, P], U32, name="w4_first_codes", align_bytes=64)
+        first_scales = keep.tile([P, P], U8, name="w4_first_scales", align_bytes=64)
+        nc.vector.quantize_mx(out=first_codes[:].bitcast(FP8X4), scales=first_scales[:], in_=w4_dealt[:, WHOLE])
 
-        z = keep.tile([P, S * PACK], BF16, name="z", align_bytes=64)
         z_codes = keep.tile([P, S], U32, name="z_codes", align_bytes=64)
         z_scales = keep.tile([P, S], U8, name="z_scales", align_bytes=64)
-        halves = [slice(0, S // 2), slice(S // 2, S)]
-        for cols in halves:
+        z = [keep.tile([P, PACK * (c.stop - c.start)], BF16, name="z%d" % part, align_bytes=64) for part, c in enumerate(Z_PARTS)]
+
+        def z_sum(part):
+            places = Z_PARTS[part]
             nc.vector.tensor_tensor(
-                z[:, PACK * cols.start : PACK * cols.stop].rearrange("p (c i t) -> p c t i", i=4, t=PACK),
-                term_a[:, :, cols].rearrange("p t (c i) -> p c t i", i=4),
-                term_b[:, :, cols].rearrange("p t (c i) -> p c t i", i=4),
+                z[part][:].rearrange("p (c i t) -> p c t i", i=2, t=PACK),
+                term_a[:, :, places].rearrange("p t (c i) -> p c t i", i=2),
+                term_b[:, :, places].rearrange("p t (c i) -> p c t i", i=2),
                 ALU.add,
             )
-        for cols in halves:
+
+        def z_quantize(part):
+            places = Z_PARTS[part]
+            nc.vector.quantize_mx(out=z_codes[:, places].bitcast(FP8X4), scales=z_scales[:, places], in_=z[part][:])
+
+        z_sum(0)
+        z_quantize(0)
+        z_sum(1)
+        z_sum(2)
+        z_quantize(1)
+        z_quantize(2)
+
+        rest_codes = keep.tile([P, S - P], U32, name="z2", align_bytes=64)
+        rest_scales = keep.tile([P, S - P], U8, name="w4_rest_scales", align_bytes=64)
+        for first, end in ((1, 2), (2, PACK)):
+            words = slice((first - 1) * P, (end - 1) * P)
             nc.vector.quantize_mx(
-                out=z_codes[:, cols].bitcast(FP8X4), scales=z_scales[:, cols], in_=z[:, PACK * cols.start : PACK * cols.stop]
+                out=rest_codes[:, words].bitcast(FP8X4), scales=rest_scales[:, words], in_=w4_dealt[:, first * S : end * S]
             )
+        w4_codes = [first_codes[:]] + [rest_codes[:, (t - 1) * P : t * P] for t in range(1, PACK)]
+        w4_scales = [first_scales[:]] + [rest_scales[:, (t - 1) * P : t * P] for t in range(1, PACK)]
+
+        h_own = [keep.tile([P, S], F32, name="h_own%d" % t) for t in range(PACK)]
+        h_products = [(0, places) for places in Z_PARTS] + [(t, WHOLE) for t in range(1, PACK)]
+        h_banks = [(psum_pairs, "h_acc")] * 2 + [(psum_single, "y_acc"), (psum_single, "h1_acc")] + [(psum_pairs, "b_acc")] * 2
+        for (t, places), (pool, bank) in zip(h_products, h_banks):
+            h_acc = pool.tile([P, S], F32, name=bank)
+            width = places.stop - places.start
+            nc.tensor.matmul_mx(
+                out=h_acc[:, 0:width],
+                lhsT=w4_codes[t].bitcast(FP8X4),
+                lhsT_scale=w4_scales[t],
+                rhs=z_codes[:, places].bitcast(FP8X4),
+                rhs_scale=z_scales[:, places],
+                start=True,
+                stop=True,
+            )
+            move = nc.vector.tensor_copy if places == Z_PARTS[-1] else nc.scalar.copy
+            move(out=h_win[t][:, places], in_=h_acc[:, 0:width])
+            move(out=h_own[t][:, places], in_=h_acc[:, 0:width])
 
         out_rows = out.rearrange("(p t) j -> p t j", t=PACK)
         for t in range(PACK):
-            h_own = ring.tile([P, S], F32, name="h_own")
-            for cols in halves if t == 0 else [lo]:
-                h_acc = psum.tile([P, S], F32, name="h_acc")
-                width = cols.stop - cols.start
-                nc.tensor.matmul_mx(
-                    out=h_acc[:, 0:width],
-                    lhsT=w4_q[0][:, t * P : (t + 1) * P].bitcast(FP8X4),
-                    lhsT_scale=w4_q[1][:, t * P : (t + 1) * P],
-                    rhs=z_codes[:, cols].bitcast(FP8X4),
-                    rhs_scale=z_scales[:, cols],
-                    start=True,
-                    stop=True,
-                )
-                nc.scalar.copy(out=h_win[t][:, cols], in_=h_acc[:, 0:width])
-                nc.scalar.copy(out=h_own[:, cols], in_=h_acc[:, 0:width])
+            pieces = HALVES if t >= PACK - 2 else [WHOLE]
             step_a = ring.tile([P, S], F32, name="step_a")
-            step_b = ring.tile([P, S], F32, name="step_b")
-            nc.vector.tensor_tensor(step_a[:], h_win[t][:].indirect(n6_l[:]), h_own[:], ALU.subtract)
-            nc.vector.tensor_tensor(step_b[:], h_win[t][:].indirect(n7_l[:]), h_own[:], ALU.subtract)
+            step_c = ring.tile([P, S], F32, name="step_c")
+            nc.vector.tensor_tensor(step_a[:], h_win[t][:].indirect(n6_l[:]), h_own[t][:], ALU.subtract)
+            for places in pieces:
+                nc.vector.tensor_tensor(
+                    step_c[:, places], h_win[t][:].indirect(entries(n7_l, places)), h_own[t][:, places], ALU.subtract
+                )
             upper = ring.tile([P, S], F32, name="upper")
-            middle = ring.tile([P, S], F32, name="middle")
-            result = ring.tile([P, S], F32, name="result")
-            pieces = halves if t == PACK - 1 else [lo]
-            for cols in pieces:
-                nc.vector.scalar_tensor_tensor(upper[:, cols], step_a[:, cols], 0.0, step_b[:, cols], ALU.max, ALU.min)
-            for cols in pieces:
-                nc.vector.scalar_tensor_tensor(middle[:, cols], step_a[:, cols], 0.0, upper[:, cols], ALU.min, ALU.max)
-            for cols in pieces:
-                nc.vector.tensor_tensor(result[:, cols], middle[:, cols], h_own[:, cols], ALU.add)
-                nc.sync.dma_start(out=out_rows[:, t, cols], in_=result[:, cols])
+            middle = keep.tile([P, S], F32, name="middle%d" % t)
+            result = keep.tile([P, S], F32, name="result%d" % t)
+            for places in pieces:
+                nc.vector.scalar_tensor_tensor(upper[:, places], step_a[:, places], 0.0, step_c[:, places], ALU.max, ALU.min)
+            for places in pieces:
+                nc.vector.scalar_tensor_tensor(middle[:, places], step_a[:, places], 0.0, upper[:, places], ALU.min, ALU.max)
+            for places in HALVES:
+                if t == PACK - 1:
+                    nc.vector.tensor_tensor(result[:, places], middle[:, places], h_own[t][:, places], ALU.add)
+                else:
+                    blocks = [slice(c, c + P) for c in range(places.start, places.stop, P)]
+                    turned = psum_pairs.tile([P, S // 2], F32, name="d_acc")
+                    for index, block in enumerate(blocks):
+                        group = turned[:, index * P : (index + 1) * P]
+                        nc.tensor.matmul(group, h_own[t][:, block], identity[:], start=True, stop=False, is_transpose=True)
+                        nc.tensor.matmul(group, middle[:, block], identity[:], start=False, stop=True, is_transpose=True)
+                    turned_sum = ring.tile([P, S // 2], F32, name="turned_sum")
+                    nc.scalar.copy(out=turned_sum[:], in_=turned[:])
+                    back = psum_pairs.tile([P, S // 2], F32, name="h_acc")
+                    for index in range(len(blocks)):
+                        square = slice(index * P, (index + 1) * P)
+                        nc.tensor.transpose(back[:, square], turned_sum[:, square], identity[:])
+                    nc.scalar.copy(out=result[:, places], in_=back[:])
+                nc.sync.dma_start(out=out_rows[:, t, places], in_=result[:, places])

@@ -91,6 +91,9 @@ def tile_picked_triogatebflowbmed_none_p_kernel(
 
         byte_table = keep.tile([P, T], U8, name="byte_table")
         nc.gpsimd.memset(byte_table[:].bitcast(I32), 0)
+        warm = keep.tile([P, 2], F32, name="warm")
+        nc.gpsimd.memset(warm[:, 0:1], 0.0)
+        nc.scalar.activation(out=warm[:, 1:2], in_=warm[:, 0:1], func=ACT.Sigmoid)
         identity = keep.tile([P, P], F32, name="identity")
         make_identity(nc, identity[:])
 

from contextlib import ExitStack

import concourse.mybir as mybir
from concourse.masks import make_identity

F32 = mybir.dt.float32
BF16 = mybir.dt.bfloat16
I32 = mybir.dt.int32
U32 = mybir.dt.uint32
U16 = mybir.dt.uint16
U8 = mybir.dt.uint8
FP8X4 = mybir.dt.float8_e4m3fn_x4
ALU = mybir.AluOpType
ACT = mybir.ActivationFunctionType

P = 128
PACK = 4
T = 2048
S = 512
STRIPE = 16
QUADRANT = 32
FLOPS = 4 * 2 * S * S * S

WHOLE = slice(0, S)
SPARE = slice(S, 2 * S)
HALVES = [slice(0, S // 2), slice(S // 2, S)]
Z_PARTS = [slice(0, 256), slice(256, 384), slice(384, S)]


def tile_picked_triogatebflowbmed_none_p_kernel(
    tc, x_words, x_scales, w1, w2, w3, gn, w4, offs, two, three, n1, n2, n3, n4, n5, n6, n7, out
):
    nc = tc.nc
    with ExitStack() as ctx:
        lists = ctx.enter_context(tc.tile_pool(name="lists", bufs=1))
        keep = ctx.enter_context(tc.tile_pool(name="keep", bufs=1))
        ring = ctx.enter_context(tc.tile_pool(name="ring", bufs=2))
        psum_pairs = ctx.enter_context(tc.psum_pool(name="psum_pairs", bufs=2))
        psum_single = ctx.enter_context(tc.psum_pool(name="psum_single", bufs=1))

        def load_list(source, name):
            tile = lists.tile([P, S // STRIPE], U16, name=name)
            nc.sync.dma_start(tile[:], source)
            return tile

        def entries(list_tile, places):
            return list_tile[:, places.start // STRIPE : places.stop // STRIPE]

        def load_weight(source, name, parts):
            rows = source.rearrange("(p j) c -> p j c", j=PACK)
            width = S // parts
            raws = []
            for part in range(parts):
                raw = keep.tile([P, PACK, width], F32, name="%s_raw%d" % (name, part), align_bytes=64)
                nc.sync.dma_start(out=raw[:], in_=rows[:, :, part * width : (part + 1) * width])
                raws.append(raw)
            return raws

        def deal_part(dealt, raws, part):
            span = P // len(raws)
            nc.scalar.copy(
                out=dealt[:].rearrange("p (t m j) -> p m j t", t=PACK, j=PACK)[:, part * span : (part + 1) * span],
                in_=raws[part][:].rearrange("p j (m t) -> p m j t", t=PACK),
            )

        def deal_weight(raws, name):
            dealt = keep.tile([P, PACK * S], BF16, name=name + "_dealt", align_bytes=64)
            for part in range(len(raws)):
                deal_part(dealt, raws, part)
            return dealt

        def quantize(values, name):
            codes = keep.tile([P, S], U32, name=name + "_codes", align_bytes=64)
            scales = keep.tile([P, S], U8, name=name + "_scales", align_bytes=64)
            nc.vector.quantize_mx(out=codes[:].bitcast(FP8X4), scales=scales[:], in_=values[:])
            return codes, scales

        def product(weight, picked, t, pool, bank):
            acc = pool.tile([P, S], F32, name=bank)
            cols = slice(t * P, (t + 1) * P)
            nc.tensor.matmul_mx(
                out=acc[:],
                lhsT=weight[0][:, cols].bitcast(FP8X4),
                lhsT_scale=weight[1][:, cols],
                rhs=picked[0][:].bitcast(FP8X4),
                rhs_scale=picked[1][:],
                start=True,
                stop=True,
            )
            return acc

        byte_table = keep.tile([P, T], U8, name="byte_table")
        nc.gpsimd.memset(byte_table[:].bitcast(I32), 0)
        warm = keep.tile([P, 2], F32, name="warm")
        nc.gpsimd.memset(warm[:, 0:1], 0.0)
        nc.scalar.activation(out=warm[:, 1:2], in_=warm[:, 0:1], func=ACT.Sigmoid)
        identity = keep.tile([P, P], F32, name="identity")
        make_identity(nc, identity[:])

        two_l = load_list(two, "two_l")
        offs_l = load_list(offs, "offs_l")
        for q in range(P // QUADRANT):
            nc.sync.dma_start(
                out=byte_table[QUADRANT * q : QUADRANT * q + PACK, :].bitcast(I32),
                in_=x_scales[0, PACK * q : PACK * (q + 1), :].bitcast(I32),
            )
        three_l = load_list(three, "three_l")
        w2_raw = load_weight(w2, "w2", 2)
        word_table = keep.tile([P, T], I32, name="word_table")
        nc.sync.dma_start(out=word_table[:], in_=x_words[0].rearrange("p n r -> p (n r)").bitcast(I32))
        w1_raw = load_weight(w1, "w1", 2)
        n2_l = load_list(n2, "n2_l")
        n1_l = load_list(n1, "n1_l")
        w3_raw = load_weight(w3, "w3", 2)
        n4_l = load_list(n4, "n4_l")
        n3_l = load_list(n3, "n3_l")
        n5_l = load_list(n5, "n5_l")
        gain = keep.tile([P, PACK], F32, name="gain")
        nc.sync.dma_start(out=gain[:], in_=gn.rearrange("(p t) o -> p (t o)", t=PACK))
        w4_raw = load_weight(w4, "w4", 1)
        n6_l = load_list(n6, "n6_l")
        n7_l = load_list(n7, "n7_l")

        def pick_bytes(list_tile, name):
            picked = keep.tile([P, S], U8, name=name + "_bytes", align_bytes=64)
            nc.vector.tensor_copy(picked[:], byte_table[:].indirect(list_tile[:]))
            return picked

        def pick_words(list_tile, name):
            picked = keep.tile([P, S], U32, name=name + "_words", align_bytes=64)
            nc.vector.tensor_copy(picked[:], word_table[:].bitcast(U32).indirect(list_tile[:]))
            return picked

        bytes_two = pick_bytes(two_l, "two")
        bytes_offs = pick_bytes(offs_l, "offs")
        bytes_three = pick_bytes(three_l, "three")
        w2_q = quantize(deal_weight(w2_raw, "w2"), "w2")
        x_two = (pick_words(two_l, "two"), bytes_two)
        x_offs = (pick_words(offs_l, "offs"), bytes_offs)
        x_three = (pick_words(three_l, "three"), bytes_three)
        w1_q = quantize(deal_weight(w1_raw, "w1"), "w1")

        y_win = [keep.tile([P, 2 * S], F32, name="y_win%d" % t, align_bytes=64) for t in range(PACK)]
        m_win = [keep.tile([P, 2 * S], F32, name="m_win%d" % t) for t in range(PACK)]
        b_win = [keep.tile([P, 2 * S], F32, name="b_win%d" % t) for t in range(PACK)]
        h_win = [keep.tile([P, 2 * S], F32, name="h_win%d" % t) for t in range(PACK)]
        pull3 = [keep.tile([P, S], F32, name="pull3_%d" % t) for t in range(PACK)]
        term_a = keep.tile([P, PACK, S], F32, name="term_a")
        term_b = keep.tile([P, PACK, S], F32, name="term_b")
        d_slots = ["w1_raw1", "w1_dealt", "d_win2", "d_win3"]

        def gate(t):
            d_acc = product(w2_q, x_two, t, psum_pairs, "d_acc")
            y_acc = product(w1_q, x_offs, t, psum_single, "y_acc")
            d_win = keep.tile([P, S], F32, name=d_slots[t], align_bytes=64)
            nc.scalar.copy(out=d_win[:], in_=d_acc[:])
            for places in HALVES:
                nc.scalar.activation(
                    out=y_win[t][:, S + places.start : S + places.stop],
                    in_=d_win[:].indirect(entries(n2_l, places)),
                    func=ACT.Sigmoid,
                )
            if t == 0:
                nc.vector.tensor_scalar(y_win[t][:, WHOLE], y_acc[:], -0.25, None, ALU.mult)
            else:
                nc.scalar.activation(out=y_win[t][:, WHOLE], in_=y_acc[:], func=ACT.Copy, scale=-0.25)
            for places in HALVES if t < 2 else [WHOLE]:
                spare = slice(S + places.start, S + places.stop)
                nc.vector.scalar_tensor_tensor(m_win[t][:, spare], y_acc[:, places], 0.5, y_win[t][:, spare], ALU.mult, ALU.mult)
            nc.vector.tensor_tensor(m_win[t][:, WHOLE], y_win[t][:].indirect(n1_l[:]), m_win[t][:, SPARE], ALU.add)

        def pulls(t):
            nc.scalar.copy(out=b_win[t][:, SPARE], in_=m_win[t][:, WHOLE])
            nc.vector.tensor_tensor(h_win[t][:, SPARE], m_win[t][:].indirect(n4_l[:]), b_win[t][:, SPARE], ALU.subtract)
            nc.vector.tensor_tensor(pull3[t][:], m_win[t][:].indirect(n3_l[:]), b_win[t][:, SPARE], ALU.subtract)

        def terms(t):
            b_acc = product(w3_q, x_three, t, psum_pairs, "b_acc")
            nc.scalar.activation(out=b_win[t][:, WHOLE], in_=b_acc[:], func=ACT.Copy, scale=gain[:, t : t + 1])
            nc.vector.tensor_tensor(term_b[:, t, :], b_win[t][:].indirect(n5_l[:]), h_win[t][:, SPARE], ALU.mult)
            nc.vector.scalar_tensor_tensor(term_a[:, t, :], pull3[t][:], 2.0, b_win[t][:, WHOLE], ALU.mult, ALU.mult)

        gate(0)
        gate(1)
        w3_dealt = keep.tile([P, PACK * S], BF16, name="y_win0", align_bytes=64)
        pulls(0)
        deal_part(w3_dealt, w3_raw, 0)
        pulls(1)
        deal_part(w3_dealt, w3_raw, 1)
        w3_q = quantize(w3_dealt, "w3")
        gate(2)
        terms(0)
        terms(1)
        gate(3)
        pulls(2)
        terms(2)
        pulls(3)
        terms(3)
        w4_dealt = keep.tile([P, PACK * S], BF16, name="y_win3", align_bytes=64)
        deal_part(w4_dealt, w4_raw, 0)
        first_codes = keep.tile([P, P], U32, name="w4_first_codes", align_bytes=64)
        first_scales = keep.tile([P, P], U8, name="w4_first_scales", align_bytes=64)
        nc.vector.quantize_mx(out=first_codes[:].bitcast(FP8X4), scales=first_scales[:], in_=w4_dealt[:, WHOLE])

        z_codes = keep.tile([P, S], U32, name="z_codes", align_bytes=64)
        z_scales = keep.tile([P, S], U8, name="z_scales", align_bytes=64)
        z = [keep.tile([P, PACK * (c.stop - c.start)], BF16, name="z%d" % part, align_bytes=64) for part, c in enumerate(Z_PARTS)]

        def z_sum(part):
            places = Z_PARTS[part]
            nc.vector.tensor_tensor(
                z[part][:].rearrange("p (c i t) -> p c t i", i=2, t=PACK),
                term_a[:, :, places].rearrange("p t (c i) -> p c t i", i=2),
                term_b[:, :, places].rearrange("p t (c i) -> p c t i", i=2),
                ALU.add,
            )

        def z_quantize(part):
            places = Z_PARTS[part]
            nc.vector.quantize_mx(out=z_codes[:, places].bitcast(FP8X4), scales=z_scales[:, places], in_=z[part][:])

        z_sum(0)
        z_quantize(0)
        z_sum(1)
        z_sum(2)
        z_quantize(1)
        z_quantize(2)

        rest_codes = keep.tile([P, S - P], U32, name="z2", align_bytes=64)
        rest_scales = keep.tile([P, S - P], U8, name="w4_rest_scales", align_bytes=64)
        for first, end in ((1, 2), (2, PACK)):
            words = slice((first - 1) * P, (end - 1) * P)
            nc.vector.quantize_mx(
                out=rest_codes[:, words].bitcast(FP8X4), scales=rest_scales[:, words], in_=w4_dealt[:, first * S : end * S]
            )
        w4_codes = [first_codes[:]] + [rest_codes[:, (t - 1) * P : t * P] for t in range(1, PACK)]
        w4_scales = [first_scales[:]] + [rest_scales[:, (t - 1) * P : t * P] for t in range(1, PACK)]

        h_own = [keep.tile([P, S], F32, name="h_own%d" % t) for t in range(PACK)]
        h_products = [(0, places) for places in Z_PARTS] + [(t, WHOLE) for t in range(1, PACK)]
        h_banks = [(psum_pairs, "h_acc")] * 2 + [(psum_single, "y_acc"), (psum_single, "h1_acc")] + [(psum_pairs, "b_acc")] * 2
        for (t, places), (pool, bank) in zip(h_products, h_banks):
            h_acc = pool.tile([P, S], F32, name=bank)
            width = places.stop - places.start
            nc.tensor.matmul_mx(
                out=h_acc[:, 0:width],
                lhsT=w4_codes[t].bitcast(FP8X4),
                lhsT_scale=w4_scales[t],
                rhs=z_codes[:, places].bitcast(FP8X4),
                rhs_scale=z_scales[:, places],
                start=True,
                stop=True,
            )
            move = nc.vector.tensor_copy if places == Z_PARTS[-1] else nc.scalar.copy
            move(out=h_win[t][:, places], in_=h_acc[:, 0:width])
            move(out=h_own[t][:, places], in_=h_acc[:, 0:width])

        out_rows = out.rearrange("(p t) j -> p t j", t=PACK)
        for t in range(PACK):
            pieces = HALVES if t >= PACK - 2 else [WHOLE]
            step_a = ring.tile([P, S], F32, name="step_a")
            step_c = ring.tile([P, S], F32, name="step_c")
            nc.vector.tensor_tensor(step_a[:], h_win[t][:].indirect(n6_l[:]), h_own[t][:], ALU.subtract)
            for places in pieces:
                nc.vector.tensor_tensor(
                    step_c[:, places], h_win[t][:].indirect(entries(n7_l, places)), h_own[t][:, places], ALU.subtract
                )
            upper = ring.tile([P, S], F32, name="upper")
            middle = keep.tile([P, S], F32, name="middle%d" % t)
            result = keep.tile([P, S], F32, name="result%d" % t)
            for places in pieces:
                nc.vector.scalar_tensor_tensor(upper[:, places], step_a[:, places], 0.0, step_c[:, places], ALU.max, ALU.min)
            for places in pieces:
                nc.vector.scalar_tensor_tensor(middle[:, places], step_a[:, places], 0.0, upper[:, places], ALU.min, ALU.max)
            for places in HALVES:
                if t == PACK - 1:
                    nc.vector.tensor_tensor(result[:, places], middle[:, places], h_own[t][:, places], ALU.add)
                else:
                    blocks = [slice(c, c + P) for c in range(places.start, places.stop, P)]
                    turned = psum_pairs.tile([P, S // 2], F32, name="d_acc")
                    for index, block in enumerate(blocks):
                        group = turned[:, index * P : (index + 1) * P]
                        nc.tensor.matmul(group, h_own[t][:, block], identity[:], start=True, stop=False, is_transpose=True)
                        nc.tensor.matmul(group, middle[:, block], identity[:], start=False, stop=True, is_transpose=True)
                    turned_sum = ring.tile([P, S // 2], F32, name="turned_sum")
                    nc.scalar.copy(out=turned_sum[:], in_=turned[:])
                    back = psum_pairs.tile([P, S // 2], F32, name="h_acc")
                    for index in range(len(blocks)):
                        square = slice(index * P, (index + 1) * P)
                        nc.tensor.transpose(back[:, square], turned_sum[:, square], identity[:])
                    nc.scalar.copy(out=result[:, places], in_=back[:])
                nc.sync.dma_start(out=out_rows[:, t, places], in_=result[:, places])
